import numpy as np
import ml_dtypes


def mxq(x, axis, fmt="e4m3"):
    dtype, down = {"e4m3": (ml_dtypes.float8_e4m3fn, 7), "e5m2": (ml_dtypes.float8_e5m2, 14)}[fmt]
    v = np.moveaxis(np.asarray(x, np.float32).astype(ml_dtypes.bfloat16).astype(np.float64), axis, -1)
    blocks = v.reshape(v.shape[:-1] + (-1, 32))
    amax = np.abs(blocks).max(-1, keepdims=True)
    byte = np.maximum(np.where(amax > 0, np.frexp(amax)[1] - 1 + 127, 0) - down, 1)
    scale = np.exp2(byte - 127.0)
    codes = (blocks / scale).astype(np.float32).astype(dtype).astype(np.float64)
    return np.moveaxis((codes * scale).reshape(v.shape), -1, axis)


WIDE = False


def mx_kscale(k):
    if not WIDE:
        return np.ones(k)
    levels = np.array([10, -10, 5, -5, 0])
    if k % 512:
        return np.exp2(np.random.permutation(np.resize(levels, k // 32))).repeat(32)
    a = np.empty((k // 512, 16))
    for p in range(k // 512):
        a[p, :8] = np.random.permutation(np.resize(levels, 8))
        for g in range(8):
            far = levels[np.abs(levels - a[p, g]) >= 10]
            a[p, g + 8] = far[np.random.randint(len(far))]
    return np.exp2(a.ravel()).repeat(32)


BF16 = ml_dtypes.bfloat16


def bf(x):
    return np.asarray(x, np.float32).astype(BF16)


def f64(x):
    return np.asarray(x).astype(np.float64)


B, T, D, H, K = 2, 1024, 1024, 4, 256
E = H * K


def draw0():
    s = mx_kscale(D)
    u = mx_kscale(T)
    return {
        "x": bf(np.random.standard_normal((B, T, D)) * s),
        "wk": bf(np.random.standard_normal((D, E)) / np.sqrt(D) / s[:, None]),
        "wv": bf(np.random.standard_normal((D, E)) / np.sqrt(D) / s[:, None]),
        "dec": bf(np.random.uniform(0.3, 1.0, (B, T, H)) * u[None, :, None]),
        "beta": bf(np.random.uniform(0.5, 1.5, (B, T)) / u[None, :]),
        "gamma": bf(np.random.uniform(0.3, 0.9, (B, H))),
        "s_prev": bf(np.random.standard_normal((B, H, K, K))),
    }


def project_heads(xq, w, heads):
    b, t, _ = xq.shape
    e = w.shape[1]
    return (xq @ mxq(f64(w), 0, "e4m3")).reshape(b, t, heads, e // heads)


def core(x, wk, wv, dec, beta, gamma, s_prev):
    t = x.shape[1]
    heads = dec.shape[2]
    xq = mxq(f64(x), 2, "e4m3")
    k = project_heads(xq, wk, heads)
    v = project_heads(xq, wv, heads)
    kd = k * f64(dec)[:, :, :, None]
    vb = v * f64(beta)[:, :, None, None]
    kdq = mxq(kd.transpose(0, 2, 3, 1), 3, "e4m3")
    vbq = mxq(vb.transpose(0, 2, 1, 3), 2, "e4m3")
    m = (kdq @ vbq) / np.sqrt(t)
    return f64(gamma)[:, :, None, None] * f64(s_prev) + m


def e4m3fn_bytes(y):
    return np.clip(np.asarray(y, np.float64), -448.0, 448.0).astype(np.float32).astype(ml_dtypes.float8_e4m3fn).view(np.uint8)


def e4m3fn_values(b):
    return np.asarray(b, np.uint8).view(ml_dtypes.float8_e4m3fn).astype(np.float64)


def setup_inputs():
    d = draw0()
    x0 = np.asarray(d['x']).astype(np.float64)
    s = (np.max(np.abs(x0), axis=(0, 1), keepdims=True) / 448.0).astype(np.float32)
    out = {}
    for k, v in d.items():
        if k == 'x':
            out['x_bytes'] = e4m3fn_bytes(x0 / s.astype(np.float64))
            out['x_scale'] = s
        else:
            out[k] = v
    return out


def reference(x_bytes, x_scale, wk, wv, dec, beta, gamma, s_prev):
    return core(e4m3fn_values(x_bytes) * x_scale.astype(np.float64), wk, wv, dec, beta, gamma, s_prev)

@@ -1,0 +1,298 @@
+from contextlib import ExitStack
+
+import concourse.mybir as mybir
+from concourse.masks import make_identity
+
+B, T, D, H, K = 2, 1024, 1024, 4, 256
+E = H * K
+FLOPS = 2 * B * T * D * 2 * E + 2 * B * H * K * K * T
+
+F32 = mybir.dt.float32
+BF16 = mybir.dt.bfloat16
+U32 = mybir.dt.uint32
+U8 = mybir.dt.uint8
+FP8 = mybir.dt.float8_e4m3fn
+FP8X4 = mybir.dt.float8_e4m3fn_x4
+COPY = mybir.ActivationFunctionType.Copy
+MULT = mybir.AluOpType.mult
+ADD = mybir.AluOpType.add
+
+P = 128
+PACK = 4
+PASS = P * PACK
+GROUPS = B * T // PASS
+INV_SQRT_T = 1.0 / 32.0
+
+W_VECTOR_COLS = {0: 512, 1: 512, 2: 256, 3: 256}
+XS_LEAD = 8
+XT_LEAD = 4
+W_LEAD = 8
+STATE_LAG = 6
+S_CHUNK = 512
+
+
+def tile_yocogatedretentionchunkstate_kernel(tc, x_bytes, x_scale, wk, wv, dec, beta, gamma, s_prev, out):
+    nc = tc.nc
+    with ExitStack() as ctx:
+        keep = ctx.enter_context(tc.tile_pool(name="keep", bufs=1))
+        work = ctx.enter_context(tc.tile_pool(name="work", bufs=3))
+        psum = ctx.enter_context(tc.psum_pool(name="psum", bufs=8))
+        ctx.enter_context(tc.manual_schedule(engines={mybir.EngineType.SP}))
+
+        xb, wraw, sp = {}, {}, {}
+
+        def load_x(grp, half):
+            b, g = divmod(grp, 2)
+            xb[grp, half] = keep.tile([P, 2, D], U8, name="xbytes_%d_%d" % (grp, half))
+            rows = x_bytes[b, PASS * g : PASS * (g + 1), :].rearrange("(p t) d -> p t d", t=PACK)
+            nc.sync.dma_start(out=xb[grp, half][:], in_=rows[:, 2 * half : 2 * half + 2, :])
+
+        def load_w(c, g):
+            w = (wk, wv)[c % 2]
+            cols = slice(PASS * (c // 2), PASS * (c // 2 + 1))
+            wraw[c, g] = keep.tile([P, PACK, PASS], BF16, name="wraw_%d_%d" % (c, g))
+            nc.sync.dma_start(out=wraw[c, g][:], in_=w[PASS * g : PASS * (g + 1), cols].rearrange("(p j) n -> p j n", j=PACK))
+
+        def load_s(b):
+            sp[b] = keep.tile([P, 2 * H, K], BF16, name="sprev_%d" % b)
+            nc.sync.dma_start(out=sp[b][:], in_=s_prev[b].rearrange("h (m p) j -> p (h m) j", p=P))
+
+        scale_in = keep.tile([P, 8], F32, name="scale_in")
+        dec_in = keep.tile([P, GROUPS, PACK * H], BF16, name="dec_in")
+        beta_in = keep.tile([P, GROUPS, PACK], BF16, name="beta_in")
+        gam = keep.tile([P, B * H], BF16, name="gam")
+        nc.sync.dma_start(out=scale_in[:], in_=x_scale.rearrange("a o (n m) -> n (a o m)", m=8))
+        load_w(0, 0)
+        load_x(0, 0)
+        load_w(0, 1)
+        load_x(0, 1)
+        nc.sync.dma_start(out=dec_in[:], in_=dec.rearrange("b (g p t) h -> p (b g) (t h)", p=P, t=PACK))
+        load_w(1, 0)
+        load_w(1, 1)
+        nc.sync.dma_start(out=beta_in[:], in_=beta.rearrange("b (g p t) -> p (b g) t", p=P, t=PACK))
+        load_x(1, 0)
+        load_x(1, 1)
+        for c in (2, 3):
+            load_w(c, 0)
+            load_w(c, 1)
+        nc.sync.dma_start(out=gam[:], in_=gamma.rearrange("b h -> (b h)").partition_broadcast(P))
+        load_s(0)
+        for grp in (2, 3):
+            load_x(grp, 0)
+            load_x(grp, 1)
+        load_s(1)
+
+        ident = keep.tile([P, P], F32, name="ident")
+        make_identity(nc, ident[:])
+
+        scale_bc = keep.tile([P, D], F32, name="scale_bc")
+        scale_view = scale_bc[:].rearrange("p (n m) -> p n m", m=8)
+        for half in range(2):
+            bank = psum.tile([P, PASS], F32, name="bank")
+            for m in range(4):
+                col = 4 * half + m
+                nc.tensor.transpose(bank[:, P * m : P * (m + 1)], scale_in[:, col : col + 1].to_broadcast([P, P]), ident[:])
+            nc.scalar.activation(
+                out=scale_view[:, :, 4 * half : 4 * half + 4], in_=bank[:].rearrange("p (m n) -> p n m", m=4), func=COPY
+            )
+
+        dec32 = keep.tile([P, GROUPS * PACK * H], F32, name="dec32")
+        beta32 = keep.tile([P, GROUPS * PACK], F32, name="beta32")
+        nc.gpsimd.tensor_scalar(
+            out=dec32[:].rearrange("p (g h t) -> p g h t", h=H, t=PACK), in0=dec_in[:].rearrange("p g (t h) -> p g h t", h=H), scalar1=1.0, scalar2=0.0, op0=MULT, op1=ADD
+        )
+        nc.gpsimd.tensor_scalar(
+            out=beta32[:], in0=beta_in[:].rearrange("p g t -> p (g t)"), scalar1=INV_SQRT_T, scalar2=0.0, op0=MULT, op1=ADD
+        )
+
+        def interleave(on_vector, planes, grouped, c0, c1):
+            dst = grouped[:, PACK * c0 : PACK * c1].rearrange("p (c i t) -> p c t i", i=4, t=PACK)
+            src = planes[:, :, c0:c1].rearrange("p t (c i) -> p c t i", i=4)
+            if on_vector:
+                nc.vector.tensor_copy(out=dst, in_=src)
+            else:
+                nc.scalar.copy(out=dst, in_=src)
+
+        def quantize(grouped, name, pool, tag, bufs=1):
+            n = grouped.shape[1] // PACK
+            codes = pool.tile([P, n], U32, name=name + "_codes", tag=tag + "_codes", bufs=bufs, align_bytes=64)
+            scales = pool.tile([P, n], U8, name=name + "_scales", tag=tag + "_scales", bufs=bufs, align_bytes=64)
+            nc.vector.quantize_mx(out=codes[:].bitcast(FP8X4), scales=scales[:], in_=grouped[:])
+            return codes, scales
+
+        wq, xs, xq, planes, kvq = {}, {}, {}, {}, {}
+
+        wg, xbank, xg, kvg, sbank = {}, {}, {}, {}, {}
+
+        def w_chunks(c):
+            jobs = []
+            for g in range(2):
+                split = min(PASS, max(0, W_VECTOR_COLS[c] - PASS * g))
+                if split > 0:
+                    jobs.append((c, g, True, 0, split))
+                for c0 in range(split, PASS, S_CHUNK):
+                    jobs.append((c, g, False, c0, min(PASS, c0 + S_CHUNK)))
+            return jobs
+
+        def group_w(c, g, on_vector, c0, c1):
+            if c0 == 0:
+                wg[c, g] = work.tile([P, PACK * PASS], BF16, name="wg", bufs=4, align_bytes=64)
+            interleave(on_vector, wraw[c, g], wg[c, g], c0, c1)
+
+        def quant_w(c, g):
+            wq[c, g] = quantize(wg[c, g], "wq_%d_%d" % (c, g), keep, "wq_%d_%d" % (c, g))
+
+        def scale_x(grp, t):
+            xs[grp, t] = work.tile([P, D], BF16, name="xs", bufs=6)
+            nc.vector.tensor_tensor(
+                out=xs[grp, t][:], in0=xb[grp, t // 2][:, t % 2, :].bitcast(FP8), in1=scale_bc[:], op=MULT
+            )
+
+        def turn_x(grp, t):
+            words = xs[grp, t][:].bitcast(F32)
+            xbank[grp, t] = psum.tile([P, PASS], F32, name="bank")
+            for g in range(2):
+                for u in range(2):
+                    j = 2 * g + u
+                    nc.tensor.transpose(xbank[grp, t][:, P * j : P * (j + 1)], words[:, 256 * g + u : 256 * (g + 1) : 2], ident[:])
+
+        def copy_x(grp, t):
+            xg[grp, t] = work.tile([P, D], BF16, name="xg", bufs=4, align_bytes=64)
+            nc.scalar.copy(
+                out=xg[grp, t][:].bitcast(F32).rearrange("p (g r u) -> p g r u", g=2, u=2),
+                in_=xbank[grp, t][:].rearrange("p (g u r) -> p g r u", g=2, u=2),
+            )
+
+        def quant_x(grp, t):
+            xq[grp, t] = quantize(xg[grp, t], "xq", work, "xq", 10)
+
+        def mx(out_ap, lhs, lcols, rhs, rcols, start, stop):
+            nc.tensor.matmul_mx(
+                out=out_ap, lhsT=lhs[0][:, lcols].bitcast(FP8X4), lhsT_scale=lhs[1][:, lcols],
+                rhs=rhs[0][:, rcols].bitcast(FP8X4), rhs_scale=rhs[1][:, rcols], start=start, stop=stop,
+            )
+
+        def factor(grp, c, hh, t):
+            if c % 2 == 0:
+                col = (grp * H + c + hh) * PACK + t
+                return dec32[:, col : col + 1]
+            return beta32[:, grp * PACK + t : grp * PACK + t + 1]
+
+        def project(grp, c, t):
+            if (grp, c) not in planes:
+                planes[grp, c] = work.tile([P, 2, PACK, K], BF16, name="planes", bufs=8)
+            bank = psum.tile([P, PASS], F32, name="bank")
+            if (grp, c) == units[-1]:
+                hh = t // 2
+                for s in range(2):
+                    slot = 2 * (t % 2) + s
+                    for g in range(2):
+                        mx(bank[:, K * s : K * (s + 1)], xq[grp, slot], slice(P * g, P * (g + 1)), wq[c, g], slice(K * hh, K * (hh + 1)), g == 0, g == 1)
+                for s in range(2):
+                    slot = 2 * (t % 2) + s
+                    nc.scalar.activation(out=planes[grp, c][:, hh, slot, :], in_=bank[:, K * s : K * (s + 1)], func=COPY, scale=factor(grp, c, hh, slot))
+                return
+            for g in range(2):
+                mx(bank[:], xq[grp, t], slice(P * g, P * (g + 1)), wq[c, g], slice(0, PASS), g == 0, g == 1)
+            if c % 2 == 0:
+                for hh in range(2):
+                    nc.scalar.activation(out=planes[grp, c][:, hh, t, :], in_=bank[:, K * hh : K * (hh + 1)], func=COPY, scale=factor(grp, c, hh, t))
+            else:
+                nc.scalar.activation(
+                    out=planes[grp, c][:, :, t, :], in_=bank[:].rearrange("p (h n) -> p h n", h=2), func=COPY, scale=factor(grp, c, 0, t)
+                )
+
+        def group_kv(grp, c, hh):
+            kvg[grp, c, hh] = work.tile([P, PACK * K], BF16, name="kvg", bufs=6, align_bytes=64)
+            nc.vector.tensor_copy(
+                out=kvg[grp, c, hh][:].rearrange("p (c i t) -> p c t i", i=4, t=PACK),
+                in_=planes[grp, c][:, hh, :, :].rearrange("p t (c i) -> p c t i", i=4),
+            )
+
+        def quant_kv(grp, c, hh):
+            kvq[grp, c, hh] = quantize(kvg[grp, c, hh], "kvq", work, "kvq", 20)
+
+        def state(b, h):
+            hp, hh = divmod(h, 2)
+            sbank[b, h] = psum.tile([P, PASS], F32, name="bank")
+            for m in range(2):
+                for g in range(2):
+                    mx(sbank[b, h][:, K * m : K * (m + 1)], kvq[2 * b + g, 2 * hp, hh], slice(P * m, P * (m + 1)),
+                       kvq[2 * b + g, 2 * hp + 1, hh], slice(0, K), g == 0, g == 1)
+
+        def blend(b, h):
+            res = work.tile([P, 2 * K], F32, name="res", bufs=4)
+            col = b * H + h
+            nc.vector.scalar_tensor_tensor(
+                out=res[:], in0=sp[b][:, 2 * h : 2 * h + 2, :].rearrange("p m j -> p (m j)"), scalar=gam[:, col : col + 1],
+                in1=sbank[b, h][:], op0=MULT, op1=ADD,
+            )
+            nc.sync.dma_start(out=out[b, h].rearrange("(m p) j -> p m j", p=P), in_=res[:].rearrange("p (m j) -> p m j", m=2))
+
+        units = [(g, 2 * hp + kind) for hp in range(2) for g in range(2) for kind in range(2)]
+        units = units + [(2 + g, c) for g in range(2) for c in range(4)]
+        ticks = []
+        for u in range(0, len(units), 2):
+            if False:
+                ticks = ticks + [(units[u + kind], t) for t in range(PACK) for kind in range(2)]
+            else:
+                ticks = ticks + [(units[u + kind], t) for kind in range(2) for t in range(PACK)]
+        first_x = {(grp, t): min(n for n in range(len(ticks)) if ticks[n][0][0] == grp and ticks[n][1] == t) for grp in range(GROUPS) for t in range(PACK)}
+        first_w = {c: min(n for n in range(len(ticks)) if ticks[n][0][1] == c) for c in range(4)}
+        last_of = {un: max(n for n in range(len(ticks)) if ticks[n][0] == un) for un in units}
+        plan = {}
+
+        def at(tick, job, *args):
+            plan.setdefault(tick, []).append((job, args))
+
+        for c in (2, 3):
+            for n, chunk in enumerate(w_chunks(c)):
+                at(first_w[c] - W_LEAD + 0 * n, group_w, *chunk)
+            for g in range(2):
+                at(first_w[c] - 2 + g - 1, quant_w, c, g)
+        for grp in range(1, GROUPS):
+            for t in range(PACK):
+                need = first_x[grp, t - t % 2]
+                at(need - XS_LEAD + 2 * (t % 2), scale_x, grp, t)
+                at(need - XT_LEAD, turn_x, grp, t)
+                at(need - XT_LEAD + 0 + t % 2, copy_x, grp, t)
+                at(need - XT_LEAD + 2 + t % 2, quant_x, grp, t)
+        for tick, ((grp, c), t) in enumerate(ticks):
+            at(tick, project, grp, c, t)
+        for grp, c in units:
+            done = last_of[grp, c] + 4
+            if (grp, c) == units[-1]:
+                done = last_of[grp, c] - 2
+            for hh in range(2):
+                at(done + 2 * hh, group_kv, grp, c, hh)
+                at(done + 2 * hh + 1, quant_kv, grp, c, hh)
+                if grp % 2 == 1 and c % 2 == 1:
+                    at(done + 2 * hh + 1 + STATE_LAG, state, grp // 2, c - 1 + hh)
+                    at(done + 2 * hh + 1 + STATE_LAG + 2, blend, grp // 2, c - 1 + hh)
+
+        w0, w1 = w_chunks(0), w_chunks(1)
+        for chunk in w0:
+            group_w(*chunk)
+        scale_x(0, 0)
+        quant_w(0, 0)
+        scale_x(0, 1)
+        turn_x(0, 0)
+        copy_x(0, 0)
+        for chunk in w1:
+            group_w(*chunk)
+        quant_w(0, 1)
+        quant_x(0, 0)
+        turn_x(0, 1)
+        copy_x(0, 1)
+        scale_x(0, 2)
+        quant_w(1, 0)
+        quant_w(1, 1)
+        quant_x(0, 1)
+        scale_x(0, 3)
+        for t in (2, 3):
+            at(first_x[0, t] - 3, turn_x, 0, t)
+            at(first_x[0, t] - 3, copy_x, 0, t)
+            at(first_x[0, t] - 2, quant_x, 0, t)
+        for tick in sorted(plan):
+            for job, args in plan[tick]:
+                job(*args)

@@ -23,12 +23,9 @@ PASS = P * PACK
 GROUPS = B * T // PASS
 INV_SQRT_T = 1.0 / 32.0
 
-W_VECTOR_COLS = {0: 512, 1: 512, 2: 256, 3: 256}
-XS_LEAD = 8
-XT_LEAD = 4
-W_LEAD = 8
-STATE_LAG = 6
-S_CHUNK = 512
+W_VECTOR_COLS = {2: 512, 3: 512}
+S_CHUNK = 256
+PAIR_UNITS = ()
 
 
 def tile_yocogatedretentionchunkstate_kernel(tc, x_bytes, x_scale, wk, wv, dec, beta, gamma, s_prev, out):
@@ -37,7 +34,7 @@ def tile_yocogatedretentionchunkstate_kernel(tc, x_bytes, x_scale, wk, wv, dec, 
         keep = ctx.enter_context(tc.tile_pool(name="keep", bufs=1))
         work = ctx.enter_context(tc.tile_pool(name="work", bufs=3))
         psum = ctx.enter_context(tc.psum_pool(name="psum", bufs=8))
-        ctx.enter_context(tc.manual_schedule(engines={mybir.EngineType.SP}))
+        ctx.enter_context(tc.manual_schedule())
 
         xb, wraw, sp = {}, {}, {}
 
@@ -62,7 +59,10 @@ def tile_yocogatedretentionchunkstate_kernel(tc, x_bytes, x_scale, wk, wv, dec, 
         beta_in = keep.tile([P, GROUPS, PACK], BF16, name="beta_in")
         gam = keep.tile([P, B * H], BF16, name="gam")
         nc.sync.dma_start(out=scale_in[:], in_=x_scale.rearrange("a o (n m) -> n (a o m)", m=8))
-        load_w(0, 0)
+        first = {}
+        for half in range(2):
+            first[half] = keep.tile([P, PACK, K], BF16, name="wfirst_%d" % half)
+            nc.sync.dma_start(out=first[half][:], in_=wk[0:PASS, K * half : K * (half + 1)].rearrange("(p j) n -> p j n", j=PACK))
         load_x(0, 0)
         load_w(0, 1)
         load_x(0, 1)
@@ -105,42 +105,38 @@ def tile_yocogatedretentionchunkstate_kernel(tc, x_bytes, x_scale, wk, wv, dec, 
             out=beta32[:], in0=beta_in[:].rearrange("p g t -> p (g t)"), scalar1=INV_SQRT_T, scalar2=0.0, op0=MULT, op1=ADD
         )
 
-        def interleave(on_vector, planes, grouped, c0, c1):
-            dst = grouped[:, PACK * c0 : PACK * c1].rearrange("p (c i t) -> p c t i", i=4, t=PACK)
-            src = planes[:, :, c0:c1].rearrange("p t (c i) -> p c t i", i=4)
+        def interleave(on_vector, rows, grouped):
+            dst = grouped.rearrange("p (c i t) -> p c t i", i=4, t=PACK)
+            src = rows.rearrange("p t (c i) -> p c t i", i=4)
             if on_vector:
                 nc.vector.tensor_copy(out=dst, in_=src)
             else:
                 nc.scalar.copy(out=dst, in_=src)
 
-        def quantize(grouped, name, pool, tag, bufs=1):
+        def quantize(grouped, pool, name, bufs):
             n = grouped.shape[1] // PACK
-            codes = pool.tile([P, n], U32, name=name + "_codes", tag=tag + "_codes", bufs=bufs, align_bytes=64)
-            scales = pool.tile([P, n], U8, name=name + "_scales", tag=tag + "_scales", bufs=bufs, align_bytes=64)
-            nc.vector.quantize_mx(out=codes[:].bitcast(FP8X4), scales=scales[:], in_=grouped[:])
+            codes = pool.tile([P, n], U32, name=name + "_codes", bufs=bufs, align_bytes=64)
+            scales = pool.tile([P, n], U8, name=name + "_scales", bufs=bufs, align_bytes=64)
+            nc.vector.quantize_mx(out=codes[:].bitcast(FP8X4), scales=scales[:], in_=grouped)
             return codes, scales
 
+        def window(q, c0, c1):
+            return q[0][:, c0:c1], q[1][:, c0:c1]
+
         wq, xs, xq, planes, kvq = {}, {}, {}, {}, {}
-
         wg, xbank, xg, kvg, sbank = {}, {}, {}, {}, {}
-
-        def w_chunks(c):
-            jobs = []
-            for g in range(2):
-                split = min(PASS, max(0, W_VECTOR_COLS[c] - PASS * g))
-                if split > 0:
-                    jobs.append((c, g, True, 0, split))
-                for c0 in range(split, PASS, S_CHUNK):
-                    jobs.append((c, g, False, c0, min(PASS, c0 + S_CHUNK)))
-            return jobs
+        WIDE = PACK * PASS
 
         def group_w(c, g, on_vector, c0, c1):
-            if c0 == 0:
-                wg[c, g] = work.tile([P, PACK * PASS], BF16, name="wg", bufs=4, align_bytes=64)
-            interleave(on_vector, wraw[c, g], wg[c, g], c0, c1)
+            if c not in wg:
+                wg[c] = work.tile([P, 2 * WIDE], BF16, name="wg", bufs=2, align_bytes=64)
+            rows = first[c0 // K][:] if (c, g) == (0, 0) else wraw[c, g][:, :, c0:c1]
+            interleave(on_vector, rows, wg[c][:, WIDE * g + PACK * c0 : WIDE * g + PACK * c1])
 
-        def quant_w(c, g):
-            wq[c, g] = quantize(wg[c, g], "wq_%d_%d" % (c, g), keep, "wq_%d_%d" % (c, g))
+        def quant_w(c, passes):
+            q = quantize(wg[c][:, WIDE * passes[0] : WIDE * (passes[-1] + 1)], keep, "wq_%d_%d" % (c, passes[0]), 1)
+            for n, g in enumerate(passes):
+                wq[c, g] = window(q, PASS * n, PASS * (n + 1))
 
         def scale_x(grp, t):
             xs[grp, t] = work.tile([P, D], BF16, name="xs", bufs=6)
@@ -148,28 +144,31 @@ def tile_yocogatedretentionchunkstate_kernel(tc, x_bytes, x_scale, wk, wv, dec, 
                 out=xs[grp, t][:], in0=xb[grp, t // 2][:, t % 2, :].bitcast(FP8), in1=scale_bc[:], op=MULT
             )
 
-        def turn_x(grp, t):
-            words = xs[grp, t][:].bitcast(F32)
-            xbank[grp, t] = psum.tile([P, PASS], F32, name="bank")
-            for g in range(2):
-                for u in range(2):
-                    j = 2 * g + u
-                    nc.tensor.transpose(xbank[grp, t][:, P * j : P * (j + 1)], words[:, 256 * g + u : 256 * (g + 1) : 2], ident[:])
+        def turn_x(grp, slots):
+            for t in slots:
+                words = xs[grp, t][:].bitcast(F32)
+                xbank[grp, t] = psum.tile([P, PASS], F32, name="bank")
+                for g in range(2):
+                    for u in range(2):
+                        j = 2 * g + u
+                        nc.tensor.transpose(xbank[grp, t][:, P * j : P * (j + 1)], words[:, 256 * g + u : 256 * (g + 1) : 2], ident[:])
+            xg[grp, slots] = work.tile([P, D * len(slots)], BF16, name="xg", bufs=3, align_bytes=64)
+            for n, t in enumerate(slots):
+                nc.scalar.copy(
+                    out=xg[grp, slots][:, D * n : D * (n + 1)].bitcast(F32).rearrange("p (g r u) -> p g r u", g=2, u=2),
+                    in_=xbank[grp, t][:].rearrange("p (g u r) -> p g r u", g=2, u=2),
+                )
 
-        def copy_x(grp, t):
-            xg[grp, t] = work.tile([P, D], BF16, name="xg", bufs=4, align_bytes=64)
-            nc.scalar.copy(
-                out=xg[grp, t][:].bitcast(F32).rearrange("p (g r u) -> p g r u", g=2, u=2),
-                in_=xbank[grp, t][:].rearrange("p (g u r) -> p g r u", g=2, u=2),
-            )
+        def quant_x(grp, slots):
+            q = quantize(xg[grp, slots][:], work, "xq", 6)
+            for n, t in enumerate(slots):
+                for g in range(2):
+                    xq[grp, t, g] = window(q, P * (2 * n + g), P * (2 * n + g + 1))
 
-        def quant_x(grp, t):
-            xq[grp, t] = quantize(xg[grp, t], "xq", work, "xq", 10)
-
-        def mx(out_ap, lhs, lcols, rhs, rcols, start, stop):
+        def mx(out_ap, lhs, rhs, start, stop):
             nc.tensor.matmul_mx(
-                out=out_ap, lhsT=lhs[0][:, lcols].bitcast(FP8X4), lhsT_scale=lhs[1][:, lcols],
-                rhs=rhs[0][:, rcols].bitcast(FP8X4), rhs_scale=rhs[1][:, rcols], start=start, stop=stop,
+                out=out_ap, lhsT=lhs[0].bitcast(FP8X4), lhsT_scale=lhs[1], rhs=rhs[0].bitcast(FP8X4), rhs_scale=rhs[1],
+                start=start, stop=stop,
             )
 
         def factor(grp, c, hh, t):
@@ -179,46 +178,56 @@ def tile_yocogatedretentionchunkstate_kernel(tc, x_bytes, x_scale, wk, wv, dec, 
             return beta32[:, grp * PACK + t : grp * PACK + t + 1]
 
         def project(grp, c, t):
-            if (grp, c) not in planes:
-                planes[grp, c] = work.tile([P, 2, PACK, K], BF16, name="planes", bufs=8)
+            if t == 0:
+                planes[grp, c] = work.tile([P, PACK, PASS], BF16, name="planes", bufs=6)
             bank = psum.tile([P, PASS], F32, name="bank")
-            if (grp, c) == units[-1]:
-                hh = t // 2
-                for s in range(2):
-                    slot = 2 * (t % 2) + s
-                    for g in range(2):
-                        mx(bank[:, K * s : K * (s + 1)], xq[grp, slot], slice(P * g, P * (g + 1)), wq[c, g], slice(K * hh, K * (hh + 1)), g == 0, g == 1)
-                for s in range(2):
-                    slot = 2 * (t % 2) + s
-                    nc.scalar.activation(out=planes[grp, c][:, hh, slot, :], in_=bank[:, K * s : K * (s + 1)], func=COPY, scale=factor(grp, c, hh, slot))
-                return
             for g in range(2):
-                mx(bank[:], xq[grp, t], slice(P * g, P * (g + 1)), wq[c, g], slice(0, PASS), g == 0, g == 1)
-            if c % 2 == 0:
-                for hh in range(2):
-                    nc.scalar.activation(out=planes[grp, c][:, hh, t, :], in_=bank[:, K * hh : K * (hh + 1)], func=COPY, scale=factor(grp, c, hh, t))
-            else:
-                nc.scalar.activation(
-                    out=planes[grp, c][:, :, t, :], in_=bank[:].rearrange("p (h n) -> p h n", h=2), func=COPY, scale=factor(grp, c, 0, t)
+                mx(bank[:], xq[grp, t, g], wq[c, g], g == 0, g == 1)
+            dst = planes[grp, c][:, t, :]
+            if units.index((grp, c)) in PAIR_UNITS:
+                dst = planes[grp, c][:].rearrange("p t n -> p (t n)").rearrange("p (u n e) -> p u e n", u=2, e=2)[:, t // 2, t % 2, :]
+            widths = (K, K) if c % 2 == 0 else (PASS,)
+            for hh, width in enumerate(widths):
+                cols = slice(width * hh, width * (hh + 1))
+                nc.scalar.activation(out=dst[:, cols], in_=bank[:, cols], func=COPY, scale=factor(grp, c, hh, t))
+
+        def project_head(grp, c, step):
+            hh, pair = divmod(step, 2)
+            if pair == 0:
+                planes[grp, c, hh] = work.tile([P, PACK, K], BF16, name="planes", bufs=6)
+            bank = psum.tile([P, PASS], F32, name="bank")
+            for s in range(2):
+                for g in range(2):
+                    mx(bank[:, K * s : K * (s + 1)], xq[grp, 2 * pair + s, g], window(wq[c, g], K * hh, K * (hh + 1)), g == 0, g == 1)
+            for s in range(2):
+                t = 2 * pair + s
+                nc.scalar.activation(out=planes[grp, c, hh][:, t, :], in_=bank[:, K * s : K * (s + 1)], func=COPY, scale=factor(grp, c, hh, t))
+
+        def group_kv(key, on_vector):
+            kvg[key] = work.tile([P, PACK * planes[key].shape[2]], BF16, name="kvg", bufs=3, align_bytes=64)
+            if len(key) == 2 and units.index(key) in PAIR_UNITS:
+                nc.vector.tensor_copy(
+                    out=kvg[key][:].bitcast(F32).rearrange("p (c i u) -> p c u i", i=4, u=2),
+                    in_=planes[key][:].rearrange("p t n -> p (t n)").bitcast(F32).rearrange("p (u c i) -> p c u i", u=2, i=4),
                 )
+            else:
+                interleave(on_vector, planes[key][:], kvg[key][:])
 
-        def group_kv(grp, c, hh):
-            kvg[grp, c, hh] = work.tile([P, PACK * K], BF16, name="kvg", bufs=6, align_bytes=64)
-            nc.vector.tensor_copy(
-                out=kvg[grp, c, hh][:].rearrange("p (c i t) -> p c t i", i=4, t=PACK),
-                in_=planes[grp, c][:, hh, :, :].rearrange("p t (c i) -> p c t i", i=4),
-            )
-
-        def quant_kv(grp, c, hh):
-            kvq[grp, c, hh] = quantize(kvg[grp, c, hh], "kvq", work, "kvq", 20)
+        def quant_kv(key):
+            q = quantize(kvg[key][:], work, "kvq", 10)
+            if len(key) == 3:
+                kvq[key] = window(q, 0, K)
+            else:
+                for hh in range(2):
+                    kvq[key + (hh,)] = window(q, K * hh, K * (hh + 1))
 
         def state(b, h):
             hp, hh = divmod(h, 2)
             sbank[b, h] = psum.tile([P, PASS], F32, name="bank")
             for m in range(2):
                 for g in range(2):
-                    mx(sbank[b, h][:, K * m : K * (m + 1)], kvq[2 * b + g, 2 * hp, hh], slice(P * m, P * (m + 1)),
-                       kvq[2 * b + g, 2 * hp + 1, hh], slice(0, K), g == 0, g == 1)
+                    mx(sbank[b, h][:, K * m : K * (m + 1)], window(kvq[2 * b + g, 2 * hp, hh], P * m, P * (m + 1)),
+                       kvq[2 * b + g, 2 * hp + 1, hh], g == 0, g == 1)
 
         def blend(b, h):
             res = work.tile([P, 2 * K], F32, name="res", bufs=4)
@@ -231,68 +240,69 @@ def tile_yocogatedretentionchunkstate_kernel(tc, x_bytes, x_scale, wk, wv, dec, 
 
         units = [(g, 2 * hp + kind) for hp in range(2) for g in range(2) for kind in range(2)]
         units = units + [(2 + g, c) for g in range(2) for c in range(4)]
-        ticks = []
-        for u in range(0, len(units), 2):
-            if False:
-                ticks = ticks + [(units[u + kind], t) for t in range(PACK) for kind in range(2)]
-            else:
-                ticks = ticks + [(units[u + kind], t) for kind in range(2) for t in range(PACK)]
-        first_x = {(grp, t): min(n for n in range(len(ticks)) if ticks[n][0][0] == grp and ticks[n][1] == t) for grp in range(GROUPS) for t in range(PACK)}
-        first_w = {c: min(n for n in range(len(ticks)) if ticks[n][0][1] == c) for c in range(4)}
-        last_of = {un: max(n for n in range(len(ticks)) if ticks[n][0] == un) for un in units}
+        first_x = {grp: PACK * min(u for u in range(len(units)) if units[u][0] == grp) for grp in range(GROUPS)}
+        first_w = {c: PACK * min(u for u in range(len(units)) if units[u][1] == c) for c in range(4)}
         plan = {}
 
         def at(tick, job, *args):
             plan.setdefault(tick, []).append((job, args))
 
-        for c in (2, 3):
-            for n, chunk in enumerate(w_chunks(c)):
-                at(first_w[c] - W_LEAD + 0 * n, group_w, *chunk)
-            for g in range(2):
-                at(first_w[c] - 2 + g - 1, quant_w, c, g)
-        for grp in range(1, GROUPS):
-            for t in range(PACK):
-                need = first_x[grp, t - t % 2]
-                at(need - XS_LEAD + 2 * (t % 2), scale_x, grp, t)
-                at(need - XT_LEAD, turn_x, grp, t)
-                at(need - XT_LEAD + 0 + t % 2, copy_x, grp, t)
-                at(need - XT_LEAD + 2 + t % 2, quant_x, grp, t)
-        for tick, ((grp, c), t) in enumerate(ticks):
-            at(tick, project, grp, c, t)
-        for grp, c in units:
-            done = last_of[grp, c] + 4
-            if (grp, c) == units[-1]:
-                done = last_of[grp, c] - 2
-            for hh in range(2):
-                at(done + 2 * hh, group_kv, grp, c, hh)
-                at(done + 2 * hh + 1, quant_kv, grp, c, hh)
-                if grp % 2 == 1 and c % 2 == 1:
-                    at(done + 2 * hh + 1 + STATE_LAG, state, grp // 2, c - 1 + hh)
-                    at(done + 2 * hh + 1 + STATE_LAG + 2, blend, grp // 2, c - 1 + hh)
-
-        w0, w1 = w_chunks(0), w_chunks(1)
-        for chunk in w0:
-            group_w(*chunk)
+        group_w(0, 0, True, 0, K)
+        group_w(0, 0, True, K, PASS)
+        group_w(0, 1, False, 0, PASS)
+        quant_w(0, (0,))
         scale_x(0, 0)
-        quant_w(0, 0)
         scale_x(0, 1)
-        turn_x(0, 0)
-        copy_x(0, 0)
-        for chunk in w1:
-            group_w(*chunk)
-        quant_w(0, 1)
-        quant_x(0, 0)
-        turn_x(0, 1)
-        copy_x(0, 1)
+        turn_x(0, (0,))
+        quant_w(0, (1,))
         scale_x(0, 2)
-        quant_w(1, 0)
-        quant_w(1, 1)
-        quant_x(0, 1)
+        quant_x(0, (0,))
+        turn_x(0, (1,))
+        group_w(1, 1, False, 0, PASS)
         scale_x(0, 3)
+        quant_x(0, (1,))
+        group_w(1, 0, True, 0, PASS)
         for t in (2, 3):
-            at(first_x[0, t] - 3, turn_x, 0, t)
-            at(first_x[0, t] - 3, copy_x, 0, t)
-            at(first_x[0, t] - 2, quant_x, 0, t)
+            at(t - 2, turn_x, 0, (t,))
+            at(t - 1, quant_x, 0, (t,))
+        at(1, quant_w, 1, (0, 1))
+        for c in (2, 3):
+            split = W_VECTOR_COLS[c]
+            if split > 0:
+                at(first_w[c] - 12, group_w, c, 0, True, 0, min(split, PASS))
+            if split > PASS:
+                at(first_w[c] - 12 + 1, group_w, c, 1, True, 0, split - PASS)
+            for n, c0 in enumerate(range(split, 2 * PASS, S_CHUNK)):
+                at(first_w[c] - 14 + 2 * n, group_w, c, c0 // PASS, False, c0 % PASS, c0 % PASS + S_CHUNK)
+            at(first_w[c] - 4, quant_w, c, (0, 1))
+        for grp in range(1, GROUPS):
+            lead, step, delay = ((6, 1, 2), (20, 4, 5), (22, 4, 5))[grp - 1]
+            start = first_x[grp] - lead
+            for t in range(PACK):
+                at(start + step * t, scale_x, grp, t)
+            for t in (0, 2):
+                turn = start + step * (t + 1) + delay
+                at(turn, turn_x, grp, (t, t + 1))
+                at(turn + 1, quant_x, grp, (t, t + 1))
+        last = len(units) - 1
+        for u, (grp, c) in enumerate(units):
+            for t in range(PACK):
+                at(PACK * u + t, project_head if u == last else project, grp, c, t)
+        for u, (grp, c) in enumerate(units):
+            if u < last:
+                done = [PACK * u + 3 + 3] * 2
+                at(done[0], group_kv, (grp, c), True)
+                at(done[0] + (5 if u < last - 1 else 2), quant_kv, (grp, c))
+            else:
+                done = [PACK * u + 2 + 1, PACK * u + 4 + 1]
+                for hh in range(2):
+                    at(done[hh], group_kv, (grp, c, hh), hh < 1)
+                    at(done[hh] + 1, quant_kv, (grp, c, hh))
+            if grp % 2 == 1 and c % 2 == 1:
+                for hh in range(2):
+                    lag = 16 if u < last - 2 else (7 if u < last else 3)
+                    at(done[hh] + lag, state, grp // 2, c - 1 + hh)
+                    at(done[hh] + lag + 1, blend, grp // 2, c - 1 + hh)
         for tick in sorted(plan):
             for job, args in plan[tick]:
                 job(*args)

@@ -23,8 +23,11 @@ PASS = P * PACK
 GROUPS = B * T // PASS
 INV_SQRT_T = 1.0 / 32.0
 
-W_VECTOR_COLS = {2: 512, 3: 512}
-S_CHUNK = 256
+X_LEAD = 21
+TURN_DELAY = 6
+W_LEAD = 14
+FINISH_LAG = 4
+STATE_LAG = 16
 PAIR_UNITS = ()
 
 
@@ -85,6 +88,9 @@ def tile_yocogatedretentionchunkstate_kernel(tc, x_bytes, x_scale, wk, wv, dec, 
         ident = keep.tile([P, P], F32, name="ident")
         make_identity(nc, ident[:])
 
+        ident_bf = keep.tile([P, P], BF16, name="ident_bf")
+        make_identity(nc, ident_bf[:])
+
         scale_bc = keep.tile([P, D], F32, name="scale_bc")
         scale_view = scale_bc[:].rearrange("p (n m) -> p n m", m=8)
         for half in range(2):
@@ -132,6 +138,18 @@ def tile_yocogatedretentionchunkstate_kernel(tc, x_bytes, x_scale, wk, wv, dec, 
                 wg[c] = work.tile([P, 2 * WIDE], BF16, name="wg", bufs=2, align_bytes=64)
             rows = first[c0 // K][:] if (c, g) == (0, 0) else wraw[c, g][:, :, c0:c1]
             interleave(on_vector, rows, wg[c][:, WIDE * g + PACK * c0 : WIDE * g + PACK * c1])
+
+        def weave_w(c, g, half):
+            if c not in wg:
+                wg[c] = work.tile([P, 2 * WIDE], BF16, name="wg", bufs=2, align_bytes=64)
+            bank = psum.tile([P, 2 * PASS], BF16, name="bank")
+            for n in range(2):
+                c0 = K * half + P * n
+                nc.tensor.matmul(
+                    bank[:, PASS * n : PASS * (n + 1)], lhsT=ident_bf[:],
+                    rhs=wraw[c, g][:, :, c0 : c0 + P].rearrange("p j n -> p n j"), start=True, stop=True,
+                )
+            nc.scalar.copy(out=wg[c][:, WIDE * g + PACK * K * half : WIDE * g + PACK * K * (half + 1)], in_=bank[:])
 
         def quant_w(c, passes):
             q = quantize(wg[c][:, WIDE * passes[0] : WIDE * (passes[-1] + 1)], keep, "wq_%d_%d" % (c, passes[0]), 1)
@@ -267,17 +285,22 @@ def tile_yocogatedretentionchunkstate_kernel(tc, x_bytes, x_scale, wk, wv, dec, 
             at(t - 1, quant_x, 0, (t,))
         at(1, quant_w, 1, (0, 1))
         for c in (2, 3):
-            split = W_VECTOR_COLS[c]
-            if split > 0:
-                at(first_w[c] - 12, group_w, c, 0, True, 0, min(split, PASS))
-            if split > PASS:
-                at(first_w[c] - 12 + 1, group_w, c, 1, True, 0, split - PASS)
-            for n, c0 in enumerate(range(split, 2 * PASS, S_CHUNK)):
-                at(first_w[c] - 14 + 2 * n, group_w, c, c0 // PASS, False, c0 % PASS, c0 % PASS + S_CHUNK)
-            at(first_w[c] - 4, quant_w, c, (0, 1))
+            start = first_w[c] - W_LEAD
+            routes = {2: "VP", 3: "PP"}[c]
+            n = 0
+            for g in range(2):
+                if routes[g] == "V":
+                    at(start + 2, group_w, c, g, True, 0, PASS)
+                for half in range(2):
+                    if routes[g] == "S":
+                        at(start + 2 * n, group_w, c, g, False, K * half, K * (half + 1))
+                        n = n + 1
+                    if routes[g] == "P":
+                        at(start + 2 * n, weave_w, c, g, half)
+                        n = n + 1
+            at(first_w[c] - PACK, quant_w, c, (0, 1))
         for grp in range(1, GROUPS):
-            lead, step, delay = ((6, 1, 2), (20, 4, 5), (22, 4, 5))[grp - 1]
-            start = first_x[grp] - lead
+            start, step, delay = (2, 1, 2) if grp == 1 else (first_x[grp] - X_LEAD, 4, TURN_DELAY)
             for t in range(PACK):
                 at(start + step * t, scale_x, grp, t)
             for t in (0, 2):
@@ -288,21 +311,28 @@ def tile_yocogatedretentionchunkstate_kernel(tc, x_bytes, x_scale, wk, wv, dec, 
         for u, (grp, c) in enumerate(units):
             for t in range(PACK):
                 at(PACK * u + t, project_head if u == last else project, grp, c, t)
-        for u, (grp, c) in enumerate(units):
-            if u < last:
-                done = [PACK * u + 3 + 3] * 2
-                at(done[0], group_kv, (grp, c), True)
-                at(done[0] + (5 if u < last - 1 else 2), quant_kv, (grp, c))
-            else:
-                done = [PACK * u + 2 + 1, PACK * u + 4 + 1]
+        for u, (grp, c) in enumerate(units[:last]):
+            done = PACK * u + 3 + FINISH_LAG
+            at(done, group_kv, (grp, c), True)
+            if u < last - 1:
+                at(done + PACK + 1, quant_kv, (grp, c))
+            if grp == 1 and c % 2 == 1:
                 for hh in range(2):
-                    at(done[hh], group_kv, (grp, c, hh), hh < 1)
-                    at(done[hh] + 1, quant_kv, (grp, c, hh))
-            if grp % 2 == 1 and c % 2 == 1:
-                for hh in range(2):
-                    lag = 16 if u < last - 2 else (7 if u < last else 3)
-                    at(done[hh] + lag, state, grp // 2, c - 1 + hh)
-                    at(done[hh] + lag + 1, blend, grp // 2, c - 1 + hh)
+                    at(done + STATE_LAG, state, 0, c - 1 + hh)
+                    at(done + STATE_LAG + 1, blend, 0, c - 1 + hh)
         for tick in sorted(plan):
             for job, args in plan[tick]:
                 job(*args)
+
+        group_kv((3, 3, 0), True)
+        quant_kv((3, 2))
+        quant_kv((3, 3, 0))
+        group_kv((3, 3, 1), False)
+        for h in range(2):
+            state(1, h)
+        for h in range(2):
+            blend(1, h)
+        quant_kv((3, 3, 1))
+        for h in range(2, H):
+            state(1, h)
+            blend(1, h)

@@ -4,8 +4,7 @@ import concourse.mybir as mybir
 from concourse.masks import make_identity
 
 B, T, D, H, K = 2, 1024, 1024, 4, 256
-E = H * K
-FLOPS = 2 * B * T * D * 2 * E + 2 * B * H * K * K * T
+FLOPS = 2 * B * T * D * 2 * H * K + 2 * B * H * K * K * T
 
 F32 = mybir.dt.float32
 BF16 = mybir.dt.bfloat16
@@ -20,319 +19,352 @@ ADD = mybir.AluOpType.add
 P = 128
 PACK = 4
 PASS = P * PACK
+PASSES = D // PASS
 GROUPS = B * T // PASS
+PACKED = PACK * PASS
+SCALES_PER_ROW = D // P
 INV_SQRT_T = 1.0 / 32.0
 
-X_LEAD = 21
-TURN_DELAY = 6
 W_LEAD = 14
+X_LEAD = 22
+TURN_DELAY = 6
 FINISH_LAG = 4
 STATE_LAG = 16
-PAIR_UNITS = ()
 
 
 def tile_yocogatedretentionchunkstate_kernel(tc, x_bytes, x_scale, wk, wv, dec, beta, gamma, s_prev, out):
     nc = tc.nc
     with ExitStack() as ctx:
         keep = ctx.enter_context(tc.tile_pool(name="keep", bufs=1))
-        work = ctx.enter_context(tc.tile_pool(name="work", bufs=3))
+        work = ctx.enter_context(tc.tile_pool(name="work", bufs=1))
         psum = ctx.enter_context(tc.psum_pool(name="psum", bufs=8))
         ctx.enter_context(tc.manual_schedule())
 
-        xb, wraw, sp = {}, {}, {}
+        x_in, w_rows, s_in = {}, {}, {}
 
-        def load_x(grp, half):
+        def load_x(grp, pair):
             b, g = divmod(grp, 2)
-            xb[grp, half] = keep.tile([P, 2, D], U8, name="xbytes_%d_%d" % (grp, half))
-            rows = x_bytes[b, PASS * g : PASS * (g + 1), :].rearrange("(p t) d -> p t d", t=PACK)
-            nc.sync.dma_start(out=xb[grp, half][:], in_=rows[:, 2 * half : 2 * half + 2, :])
+            x_in[grp, pair] = keep.tile([P, 2, D], U8, name="xbytes_%d_%d" % (grp, pair))
+            tokens = x_bytes[b, PASS * g : PASS * (g + 1), :].rearrange("(p t) d -> p t d", t=PACK)
+            nc.sync.dma_start(out=x_in[grp, pair][:], in_=tokens[:, 2 * pair : 2 * pair + 2, :])
 
-        def load_w(c, g):
-            w = (wk, wv)[c % 2]
-            cols = slice(PASS * (c // 2), PASS * (c // 2 + 1))
-            wraw[c, g] = keep.tile([P, PACK, PASS], BF16, name="wraw_%d_%d" % (c, g))
-            nc.sync.dma_start(out=wraw[c, g][:], in_=w[PASS * g : PASS * (g + 1), cols].rearrange("(p j) n -> p j n", j=PACK))
+        def load_w(blk, g, c0, c1):
+            weight, base = (wk, wv)[blk % 2], PASS * (blk // 2)
+            w_rows[blk, g, c0] = keep.tile([P, PACK, c1 - c0], BF16, name="wrows_%d_%d_%d" % (blk, g, c0))
+            src = weight[PASS * g : PASS * (g + 1), base + c0 : base + c1].rearrange("(p t) n -> p t n", t=PACK)
+            nc.sync.dma_start(out=w_rows[blk, g, c0][:], in_=src)
 
         def load_s(b):
-            sp[b] = keep.tile([P, 2 * H, K], BF16, name="sprev_%d" % b)
-            nc.sync.dma_start(out=sp[b][:], in_=s_prev[b].rearrange("h (m p) j -> p (h m) j", p=P))
+            s_in[b] = keep.tile([P, 2 * H, K], BF16, name="sprev_%d" % b)
+            nc.sync.dma_start(out=s_in[b][:], in_=s_prev[b].rearrange("h (m p) j -> p (h m) j", p=P))
 
-        scale_in = keep.tile([P, 8], F32, name="scale_in")
+        scale_in = keep.tile([P, SCALES_PER_ROW], F32, name="scale_in")
         dec_in = keep.tile([P, GROUPS, PACK * H], BF16, name="dec_in")
         beta_in = keep.tile([P, GROUPS, PACK], BF16, name="beta_in")
-        gam = keep.tile([P, B * H], BF16, name="gam")
-        nc.sync.dma_start(out=scale_in[:], in_=x_scale.rearrange("a o (n m) -> n (a o m)", m=8))
-        first = {}
-        for half in range(2):
-            first[half] = keep.tile([P, PACK, K], BF16, name="wfirst_%d" % half)
-            nc.sync.dma_start(out=first[half][:], in_=wk[0:PASS, K * half : K * (half + 1)].rearrange("(p j) n -> p j n", j=PACK))
+        gamma_in = keep.tile([P, B * H], BF16, name="gamma_in")
+        nc.sync.dma_start(out=scale_in[:], in_=x_scale.rearrange("a o (n m) -> n (a o m)", m=SCALES_PER_ROW))
+        load_w(0, 0, 0, K)
+        load_w(0, 0, K, PASS)
         load_x(0, 0)
-        load_w(0, 1)
+        load_w(0, 1, 0, PASS)
         load_x(0, 1)
         nc.sync.dma_start(out=dec_in[:], in_=dec.rearrange("b (g p t) h -> p (b g) (t h)", p=P, t=PACK))
-        load_w(1, 0)
-        load_w(1, 1)
+        load_w(1, 0, 0, PASS)
+        load_w(1, 1, 0, PASS)
         nc.sync.dma_start(out=beta_in[:], in_=beta.rearrange("b (g p t) -> p (b g) t", p=P, t=PACK))
         load_x(1, 0)
         load_x(1, 1)
-        for c in (2, 3):
-            load_w(c, 0)
-            load_w(c, 1)
-        nc.sync.dma_start(out=gam[:], in_=gamma.rearrange("b h -> (b h)").partition_broadcast(P))
+        for blk in (2, 3):
+            for g in range(PASSES):
+                load_w(blk, g, 0, PASS)
+        nc.sync.dma_start(out=gamma_in[:], in_=gamma.rearrange("b h -> (b h)").partition_broadcast(P))
         load_s(0)
         for grp in (2, 3):
             load_x(grp, 0)
             load_x(grp, 1)
         load_s(1)
 
-        ident = keep.tile([P, P], F32, name="ident")
-        make_identity(nc, ident[:])
+        ident_f32 = keep.tile([P, P], F32, name="ident_f32")
+        make_identity(nc, ident_f32[:])
+        ident_bf16 = keep.tile([P, P], BF16, name="ident_bf16")
+        make_identity(nc, ident_bf16[:])
 
-        ident_bf = keep.tile([P, P], BF16, name="ident_bf")
-        make_identity(nc, ident_bf[:])
-
-        scale_bc = keep.tile([P, D], F32, name="scale_bc")
-        scale_view = scale_bc[:].rearrange("p (n m) -> p n m", m=8)
-        for half in range(2):
+        scale_all = keep.tile([P, D], F32, name="scale_all")
+        scale_by_m = scale_all[:].rearrange("p (n m) -> p n m", m=SCALES_PER_ROW)
+        for m0 in range(0, SCALES_PER_ROW, PACK):
             bank = psum.tile([P, PASS], F32, name="bank")
-            for m in range(4):
-                col = 4 * half + m
-                nc.tensor.transpose(bank[:, P * m : P * (m + 1)], scale_in[:, col : col + 1].to_broadcast([P, P]), ident[:])
+            for m in range(PACK):
+                column = scale_in[:, m0 + m : m0 + m + 1].to_broadcast([P, P])
+                nc.tensor.transpose(bank[:, P * m : P * (m + 1)], column, ident_f32[:])
             nc.scalar.activation(
-                out=scale_view[:, :, 4 * half : 4 * half + 4], in_=bank[:].rearrange("p (m n) -> p n m", m=4), func=COPY
+                out=scale_by_m[:, :, m0 : m0 + PACK], in_=bank[:].rearrange("p (m n) -> p n m", m=PACK), func=COPY
             )
 
         dec32 = keep.tile([P, GROUPS * PACK * H], F32, name="dec32")
         beta32 = keep.tile([P, GROUPS * PACK], F32, name="beta32")
-        nc.gpsimd.tensor_scalar(
-            out=dec32[:].rearrange("p (g h t) -> p g h t", h=H, t=PACK), in0=dec_in[:].rearrange("p g (t h) -> p g h t", h=H), scalar1=1.0, scalar2=0.0, op0=MULT, op1=ADD
-        )
-        nc.gpsimd.tensor_scalar(
-            out=beta32[:], in0=beta_in[:].rearrange("p g t -> p (g t)"), scalar1=INV_SQRT_T, scalar2=0.0, op0=MULT, op1=ADD
-        )
 
-        def interleave(on_vector, rows, grouped):
-            dst = grouped.rearrange("p (c i t) -> p c t i", i=4, t=PACK)
-            src = rows.rearrange("p t (c i) -> p c t i", i=4)
-            if on_vector:
-                nc.vector.tensor_copy(out=dst, in_=src)
-            else:
-                nc.scalar.copy(out=dst, in_=src)
+        def widen_factors():
+            nc.vector.tensor_copy(
+                out=dec32[:].rearrange("p (g h t) -> p g h t", h=H, t=PACK),
+                in_=dec_in[:].rearrange("p g (t h) -> p g h t", h=H),
+            )
+            nc.vector.tensor_scalar(
+                out=beta32[:], in0=beta_in[:].rearrange("p g t -> p (g t)"), scalar1=INV_SQRT_T, scalar2=None, op0=MULT
+            )
 
-        def quantize(grouped, pool, name, bufs):
-            n = grouped.shape[1] // PACK
+        def pack(copy, rows, packed):
+            copy(
+                out=packed.rearrange("p (c i t) -> p c t i", i=4, t=PACK),
+                in_=rows.rearrange("p t (c i) -> p c t i", i=4),
+            )
+
+        def quantize(packed, pool, name, bufs):
+            n = packed.shape[1] // PACK
             codes = pool.tile([P, n], U32, name=name + "_codes", bufs=bufs, align_bytes=64)
             scales = pool.tile([P, n], U8, name=name + "_scales", bufs=bufs, align_bytes=64)
-            nc.vector.quantize_mx(out=codes[:].bitcast(FP8X4), scales=scales[:], in_=grouped)
+            nc.vector.quantize_mx(out=codes[:].bitcast(FP8X4), scales=scales[:], in_=packed)
             return codes, scales
 
-        def window(q, c0, c1):
-            return q[0][:, c0:c1], q[1][:, c0:c1]
+        def window(quantised, c0, c1):
+            return quantised[0][:, c0:c1], quantised[1][:, c0:c1]
 
-        wq, xs, xq, planes, kvq = {}, {}, {}, {}, {}
-        wg, xbank, xg, kvg, sbank = {}, {}, {}, {}, {}
-        WIDE = PACK * PASS
+        def mx_sum(out_ap, lhs_by_pass, rhs_by_pass):
+            for g, (lhs, rhs) in enumerate(zip(lhs_by_pass, rhs_by_pass)):
+                nc.tensor.matmul_mx(
+                    out=out_ap,
+                    lhsT=lhs[0].bitcast(FP8X4),
+                    lhsT_scale=lhs[1],
+                    rhs=rhs[0].bitcast(FP8X4),
+                    rhs_scale=rhs[1],
+                    start=(g == 0),
+                    stop=(g == len(lhs_by_pass) - 1),
+                )
 
-        def group_w(c, g, on_vector, c0, c1):
-            if c not in wg:
-                wg[c] = work.tile([P, 2 * WIDE], BF16, name="wg", bufs=2, align_bytes=64)
-            rows = first[c0 // K][:] if (c, g) == (0, 0) else wraw[c, g][:, :, c0:c1]
-            interleave(on_vector, rows, wg[c][:, WIDE * g + PACK * c0 : WIDE * g + PACK * c1])
+        w_packed, w_q = {}, {}
 
-        def weave_w(c, g, half):
-            if c not in wg:
-                wg[c] = work.tile([P, 2 * WIDE], BF16, name="wg", bufs=2, align_bytes=64)
+        def w_target(blk, g, c0, c1):
+            if blk not in w_packed:
+                w_packed[blk] = work.tile([P, PASSES * PACKED], BF16, name="w_packed", bufs=2, align_bytes=64)
+            return w_packed[blk][:, PACKED * g + PACK * c0 : PACKED * g + PACK * c1]
+
+        def pack_w(copy, blk, g, c0):
+            rows = w_rows[blk, g, c0]
+            pack(copy, rows[:], w_target(blk, g, c0, c0 + rows.shape[2]))
+
+        def weave_w(blk, g, half):
+            target = w_target(blk, g, K * half, K * (half + 1))
             bank = psum.tile([P, 2 * PASS], BF16, name="bank")
             for n in range(2):
                 c0 = K * half + P * n
                 nc.tensor.matmul(
-                    bank[:, PASS * n : PASS * (n + 1)], lhsT=ident_bf[:],
-                    rhs=wraw[c, g][:, :, c0 : c0 + P].rearrange("p j n -> p n j"), start=True, stop=True,
+                    bank[:, PASS * n : PASS * (n + 1)],
+                    lhsT=ident_bf16[:],
+                    rhs=w_rows[blk, g, 0][:, :, c0 : c0 + P].rearrange("p t n -> p n t"),
+                    start=True,
+                    stop=True,
                 )
-            nc.scalar.copy(out=wg[c][:, WIDE * g + PACK * K * half : WIDE * g + PACK * K * (half + 1)], in_=bank[:])
+            nc.scalar.copy(out=target, in_=bank[:])
 
-        def quant_w(c, passes):
-            q = quantize(wg[c][:, WIDE * passes[0] : WIDE * (passes[-1] + 1)], keep, "wq_%d_%d" % (c, passes[0]), 1)
+        def quantize_w(blk, passes):
+            packed = w_packed[blk][:, PACKED * passes[0] : PACKED * (passes[-1] + 1)]
+            quantised = quantize(packed, keep, "wq_%d_%d" % (blk, passes[0]), 1)
             for n, g in enumerate(passes):
-                wq[c, g] = window(q, PASS * n, PASS * (n + 1))
+                w_q[blk, g] = window(quantised, PASS * n, PASS * (n + 1))
+
+        x_scaled, x_packed, x_q = {}, {}, {}
 
         def scale_x(grp, t):
-            xs[grp, t] = work.tile([P, D], BF16, name="xs", bufs=6)
-            nc.vector.tensor_tensor(
-                out=xs[grp, t][:], in0=xb[grp, t // 2][:, t % 2, :].bitcast(FP8), in1=scale_bc[:], op=MULT
-            )
+            x_scaled[grp, t] = work.tile([P, D], BF16, name="x_scaled", bufs=6)
+            values = x_in[grp, t // 2][:, t % 2, :].bitcast(FP8)
+            nc.vector.tensor_tensor(out=x_scaled[grp, t][:], in0=values, in1=scale_all[:], op=MULT)
 
         def turn_x(grp, slots):
+            banks = []
             for t in slots:
-                words = xs[grp, t][:].bitcast(F32)
-                xbank[grp, t] = psum.tile([P, PASS], F32, name="bank")
-                for g in range(2):
+                words = x_scaled[grp, t][:].bitcast(F32)
+                bank = psum.tile([P, PASS], F32, name="bank")
+                for g in range(PASSES):
                     for u in range(2):
                         j = 2 * g + u
-                        nc.tensor.transpose(xbank[grp, t][:, P * j : P * (j + 1)], words[:, 256 * g + u : 256 * (g + 1) : 2], ident[:])
-            xg[grp, slots] = work.tile([P, D * len(slots)], BF16, name="xg", bufs=3, align_bytes=64)
-            for n, t in enumerate(slots):
+                        every_second = words[:, 2 * P * g + u : 2 * P * (g + 1) : 2]
+                        nc.tensor.transpose(bank[:, P * j : P * (j + 1)], every_second, ident_f32[:])
+                banks.append(bank)
+            x_packed[grp, slots] = work.tile([P, D * len(slots)], BF16, name="x_packed", bufs=3, align_bytes=64)
+            for n, bank in enumerate(banks):
+                target = x_packed[grp, slots][:, D * n : D * (n + 1)].bitcast(F32)
                 nc.scalar.copy(
-                    out=xg[grp, slots][:, D * n : D * (n + 1)].bitcast(F32).rearrange("p (g r u) -> p g r u", g=2, u=2),
-                    in_=xbank[grp, t][:].rearrange("p (g u r) -> p g r u", g=2, u=2),
+                    out=target.rearrange("p (g r u) -> p g r u", g=PASSES, u=2),
+                    in_=bank[:].rearrange("p (g u r) -> p g r u", g=PASSES, u=2),
                 )
 
-        def quant_x(grp, slots):
-            q = quantize(xg[grp, slots][:], work, "xq", 6)
+        def quantize_x(grp, slots):
+            quantised = quantize(x_packed[grp, slots][:], work, "x_q", 8)
             for n, t in enumerate(slots):
-                for g in range(2):
-                    xq[grp, t, g] = window(q, P * (2 * n + g), P * (2 * n + g + 1))
+                x_q[grp, t] = [window(quantised, P * (PASSES * n + g), P * (PASSES * n + g + 1)) for g in range(PASSES)]
 
-        def mx(out_ap, lhs, rhs, start, stop):
-            nc.tensor.matmul_mx(
-                out=out_ap, lhsT=lhs[0].bitcast(FP8X4), lhsT_scale=lhs[1], rhs=rhs[0].bitcast(FP8X4), rhs_scale=rhs[1],
-                start=start, stop=stop,
-            )
+        kv_rows, kv_packed, kv_q = {}, {}, {}
 
-        def factor(grp, c, hh, t):
-            if c % 2 == 0:
-                col = (grp * H + c + hh) * PACK + t
+        def factor(grp, blk, hh, t):
+            if blk % 2 == 0:
+                col = (grp * H + blk + hh) * PACK + t
                 return dec32[:, col : col + 1]
             return beta32[:, grp * PACK + t : grp * PACK + t + 1]
 
-        def project(grp, c, t):
+        def project(grp, blk, t):
             if t == 0:
-                planes[grp, c] = work.tile([P, PACK, PASS], BF16, name="planes", bufs=6)
+                kv_rows[grp, blk] = work.tile([P, PACK, PASS], BF16, name="kv_rows", bufs=7)
             bank = psum.tile([P, PASS], F32, name="bank")
-            for g in range(2):
-                mx(bank[:], xq[grp, t, g], wq[c, g], g == 0, g == 1)
-            dst = planes[grp, c][:, t, :]
-            if units.index((grp, c)) in PAIR_UNITS:
-                dst = planes[grp, c][:].rearrange("p t n -> p (t n)").rearrange("p (u n e) -> p u e n", u=2, e=2)[:, t // 2, t % 2, :]
-            widths = (K, K) if c % 2 == 0 else (PASS,)
-            for hh, width in enumerate(widths):
+            mx_sum(bank[:], x_q[grp, t], [w_q[blk, g] for g in range(PASSES)])
+            width = K if blk % 2 == 0 else PASS
+            for hh in range(PASS // width):
                 cols = slice(width * hh, width * (hh + 1))
-                nc.scalar.activation(out=dst[:, cols], in_=bank[:, cols], func=COPY, scale=factor(grp, c, hh, t))
-
-        def project_head(grp, c, step):
-            hh, pair = divmod(step, 2)
-            if pair == 0:
-                planes[grp, c, hh] = work.tile([P, PACK, K], BF16, name="planes", bufs=6)
-            bank = psum.tile([P, PASS], F32, name="bank")
-            for s in range(2):
-                for g in range(2):
-                    mx(bank[:, K * s : K * (s + 1)], xq[grp, 2 * pair + s, g], window(wq[c, g], K * hh, K * (hh + 1)), g == 0, g == 1)
-            for s in range(2):
-                t = 2 * pair + s
-                nc.scalar.activation(out=planes[grp, c, hh][:, t, :], in_=bank[:, K * s : K * (s + 1)], func=COPY, scale=factor(grp, c, hh, t))
-
-        def group_kv(key, on_vector):
-            kvg[key] = work.tile([P, PACK * planes[key].shape[2]], BF16, name="kvg", bufs=3, align_bytes=64)
-            if len(key) == 2 and units.index(key) in PAIR_UNITS:
-                nc.vector.tensor_copy(
-                    out=kvg[key][:].bitcast(F32).rearrange("p (c i u) -> p c u i", i=4, u=2),
-                    in_=planes[key][:].rearrange("p t n -> p (t n)").bitcast(F32).rearrange("p (u c i) -> p c u i", u=2, i=4),
+                nc.scalar.activation(
+                    out=kv_rows[grp, blk][:, t, cols], in_=bank[:, cols], func=COPY, scale=factor(grp, blk, hh, t)
                 )
-            else:
-                interleave(on_vector, planes[key][:], kvg[key][:])
 
-        def quant_kv(key):
-            q = quantize(kvg[key][:], work, "kvq", 10)
-            if len(key) == 3:
-                kvq[key] = window(q, 0, K)
-            else:
-                for hh in range(2):
-                    kvq[key + (hh,)] = window(q, K * hh, K * (hh + 1))
+        def project_head(grp, blk, hh, pair):
+            if pair == 0:
+                kv_rows[grp, blk, hh] = work.tile([P, PACK, K], BF16, name="kv_rows", bufs=7)
+            bank = psum.tile([P, PASS], F32, name="bank")
+            weights = [window(w_q[blk, g], K * hh, K * (hh + 1)) for g in range(PASSES)]
+            for n in range(2):
+                mx_sum(bank[:, K * n : K * (n + 1)], x_q[grp, 2 * pair + n], weights)
+            for n in range(2):
+                t = 2 * pair + n
+                nc.scalar.activation(
+                    out=kv_rows[grp, blk, hh][:, t, :],
+                    in_=bank[:, K * n : K * (n + 1)],
+                    func=COPY,
+                    scale=factor(grp, blk, hh, t),
+                )
 
-        def state(b, h):
-            hp, hh = divmod(h, 2)
-            sbank[b, h] = psum.tile([P, PASS], F32, name="bank")
-            for m in range(2):
-                for g in range(2):
-                    mx(sbank[b, h][:, K * m : K * (m + 1)], window(kvq[2 * b + g, 2 * hp, hh], P * m, P * (m + 1)),
-                       kvq[2 * b + g, 2 * hp + 1, hh], g == 0, g == 1)
+        def pack_kv(copy, key):
+            rows = kv_rows[key]
+            kv_packed[key] = work.tile([P, PACK * rows.shape[2]], BF16, name="kv_packed", bufs=3, align_bytes=64)
+            pack(copy, rows[:], kv_packed[key][:])
 
-        def blend(b, h):
-            res = work.tile([P, 2 * K], F32, name="res", bufs=4)
-            col = b * H + h
+        def quantize_kv(key):
+            quantised = quantize(kv_packed[key][:], work, "kv_q", 10)
+            heads = key[2:] if len(key) == 3 else range(2)
+            for n, hh in enumerate(heads):
+                kv_q[key[0], key[1], hh] = window(quantised, K * n, K * (n + 1))
+
+        state_bank = {}
+
+        def state(b, h, halves):
+            blk, hh = 2 * (h // 2), h % 2
+            state_bank[b, h, halves] = psum.tile([P, K * len(halves)], F32, name="bank")
+            for n, m in enumerate(halves):
+                keys = [window(kv_q[2 * b + g, blk, hh], P * m, P * (m + 1)) for g in range(2)]
+                vals = [kv_q[2 * b + g, blk + 1, hh] for g in range(2)]
+                mx_sum(state_bank[b, h, halves][:, K * n : K * (n + 1)], keys, vals)
+
+        def blend(b, h, halves):
+            first, count = halves[0], len(halves)
+            res = work.tile([P, K * count], F32, name="res", bufs=5)
+            previous = s_in[b][:, 2 * h + first : 2 * h + first + count, :].rearrange("p m j -> p (m j)")
             nc.vector.scalar_tensor_tensor(
-                out=res[:], in0=sp[b][:, 2 * h : 2 * h + 2, :].rearrange("p m j -> p (m j)"), scalar=gam[:, col : col + 1],
-                in1=sbank[b, h][:], op0=MULT, op1=ADD,
+                out=res[:],
+                in0=previous,
+                scalar=gamma_in[:, b * H + h : b * H + h + 1],
+                in1=state_bank[b, h, halves][:],
+                op0=MULT,
+                op1=ADD,
             )
-            nc.sync.dma_start(out=out[b, h].rearrange("(m p) j -> p m j", p=P), in_=res[:].rearrange("p (m j) -> p m j", m=2))
+            stored = out[b, h, P * first : P * (first + count), :].rearrange("(m p) j -> p m j", p=P)
+            nc.sync.dma_start(out=stored, in_=res[:].rearrange("p (m j) -> p m j", m=count))
+
+        on_vector, on_scalar = nc.vector.tensor_copy, nc.scalar.copy
+        both = (0, 1)
 
         units = [(g, 2 * hp + kind) for hp in range(2) for g in range(2) for kind in range(2)]
-        units = units + [(2 + g, c) for g in range(2) for c in range(4)]
-        first_x = {grp: PACK * min(u for u in range(len(units)) if units[u][0] == grp) for grp in range(GROUPS)}
-        first_w = {c: PACK * min(u for u in range(len(units)) if units[u][1] == c) for c in range(4)}
+        units = units + [(grp, blk) for grp in (2, 3) for blk in range(4)]
+        first_tick_of_group = {grp: PACK * [u[0] for u in units].index(grp) for grp in range(GROUPS)}
+        first_tick_of_block = {blk: PACK * [u[1] for u in units].index(blk) for blk in range(4)}
+        last = len(units) - 1
+
+        pack_w(on_vector, 0, 0, 0)
+        pack_w(on_vector, 0, 0, K)
+        pack_w(on_scalar, 0, 1, 0)
+        quantize_w(0, (0,))
+        scale_x(0, 0)
+        scale_x(0, 1)
+        turn_x(0, (0,))
+        quantize_w(0, (1,))
+        scale_x(0, 2)
+        quantize_x(0, (0,))
+        widen_factors()
+        turn_x(0, (1,))
+        pack_w(on_scalar, 1, 1, 0)
+        scale_x(0, 3)
+        quantize_x(0, (1,))
+        pack_w(on_vector, 1, 0, 0)
+
         plan = {}
 
         def at(tick, job, *args):
             plan.setdefault(tick, []).append((job, args))
 
-        group_w(0, 0, True, 0, K)
-        group_w(0, 0, True, K, PASS)
-        group_w(0, 1, False, 0, PASS)
-        quant_w(0, (0,))
-        scale_x(0, 0)
-        scale_x(0, 1)
-        turn_x(0, (0,))
-        quant_w(0, (1,))
-        scale_x(0, 2)
-        quant_x(0, (0,))
-        turn_x(0, (1,))
-        group_w(1, 1, False, 0, PASS)
-        scale_x(0, 3)
-        quant_x(0, (1,))
-        group_w(1, 0, True, 0, PASS)
         for t in (2, 3):
             at(t - 2, turn_x, 0, (t,))
-            at(t - 1, quant_x, 0, (t,))
-        at(1, quant_w, 1, (0, 1))
-        for c in (2, 3):
-            start = first_w[c] - W_LEAD
-            routes = {2: "VP", 3: "PP"}[c]
-            n = 0
-            for g in range(2):
-                if routes[g] == "V":
-                    at(start + 2, group_w, c, g, True, 0, PASS)
-                for half in range(2):
-                    if routes[g] == "S":
-                        at(start + 2 * n, group_w, c, g, False, K * half, K * (half + 1))
-                        n = n + 1
-                    if routes[g] == "P":
-                        at(start + 2 * n, weave_w, c, g, half)
-                        n = n + 1
-            at(first_w[c] - PACK, quant_w, c, (0, 1))
+            at(t - 1, quantize_x, 0, (t,))
+        at(1, quantize_w, 1, both)
+
+        woven = {2: (1,), 3: both}
+        at(first_tick_of_block[2] - W_LEAD + 2, pack_w, on_vector, 2, 0, 0)
+        for blk in (2, 3):
+            halves_to_weave = [(g, half) for g in woven[blk] for half in range(2)]
+            for n, (g, half) in enumerate(halves_to_weave):
+                at(first_tick_of_block[blk] - W_LEAD + 2 * n, weave_w, blk, g, half)
+            at(first_tick_of_block[blk] - PACK, quantize_w, blk, both)
+
         for grp in range(1, GROUPS):
-            start, step, delay = (2, 1, 2) if grp == 1 else (first_x[grp] - X_LEAD, 4, TURN_DELAY)
+            start, step, delay = (2, 1, 2) if grp == 1 else (first_tick_of_group[grp] - X_LEAD, PACK, TURN_DELAY)
             for t in range(PACK):
                 at(start + step * t, scale_x, grp, t)
             for t in (0, 2):
                 turn = start + step * (t + 1) + delay
                 at(turn, turn_x, grp, (t, t + 1))
-                at(turn + 1, quant_x, grp, (t, t + 1))
-        last = len(units) - 1
-        for u, (grp, c) in enumerate(units):
+                at(turn + 2, quantize_x, grp, (t, t + 1))
+
+        for u, (grp, blk) in enumerate(units[:last]):
             for t in range(PACK):
-                at(PACK * u + t, project_head if u == last else project, grp, c, t)
-        for u, (grp, c) in enumerate(units[:last]):
-            done = PACK * u + 3 + FINISH_LAG
-            at(done, group_kv, (grp, c), True)
-            if u < last - 1:
-                at(done + PACK + 1, quant_kv, (grp, c))
-            if grp == 1 and c % 2 == 1:
-                for hh in range(2):
-                    at(done + STATE_LAG, state, 0, c - 1 + hh)
-                    at(done + STATE_LAG + 1, blend, 0, c - 1 + hh)
+                at(PACK * u + t, project, grp, blk, t)
+
+        for u, (grp, blk) in enumerate(units[: last - 1]):
+            done = PACK * u + PACK - 1 + FINISH_LAG
+            at(done, pack_kv, on_vector, (grp, blk))
+            if grp < GROUPS - 1:
+                at(done + PACK + 1, quantize_kv, (grp, blk))
+            if grp == 1 and blk % 2 == 1:
+                for h in (blk - 1, blk):
+                    at(done + STATE_LAG, state, 0, h, both)
+                    at(done + STATE_LAG + 1, blend, 0, h, both)
+
         for tick in sorted(plan):
             for job, args in plan[tick]:
                 job(*args)
 
-        group_kv((3, 3, 0), True)
-        quant_kv((3, 2))
-        quant_kv((3, 3, 0))
-        group_kv((3, 3, 1), False)
+        grp = GROUPS - 1
+        quantize_kv((grp, 0))
+        project_head(grp, 3, 0, 0)
+        project_head(grp, 3, 0, 1)
+        project_head(grp, 3, 1, 0)
+        pack_kv(on_vector, (grp, 2))
+        project_head(grp, 3, 1, 1)
+        quantize_kv((grp, 1))
+        pack_kv(on_vector, (grp, 3, 0))
+        quantize_kv((grp, 2))
+        quantize_kv((grp, 3, 0))
+        pack_kv(on_scalar, (grp, 3, 1))
         for h in range(2):
-            state(1, h)
+            state(1, h, both)
         for h in range(2):
-            blend(1, h)
-        quant_kv((3, 3, 1))
-        for h in range(2, H):
-            state(1, h)
-            blend(1, h)
+            blend(1, h, both)
+        quantize_kv((grp, 3, 1))
+        state(1, 2, both)
+        blend(1, 2, both)
+        for m in range(2):
+            state(1, 3, (m,))
+        for m in range(2):
+            blend(1, 3, (m,))

from contextlib import ExitStack

import concourse.mybir as mybir
from concourse.masks import make_identity

B, T, D, H, K = 2, 1024, 1024, 4, 256
FLOPS = 2 * B * T * D * 2 * H * K + 2 * B * H * K * K * T

F32 = mybir.dt.float32
BF16 = mybir.dt.bfloat16
U32 = mybir.dt.uint32
U8 = mybir.dt.uint8
FP8 = mybir.dt.float8_e4m3fn
FP8X4 = mybir.dt.float8_e4m3fn_x4
COPY = mybir.ActivationFunctionType.Copy
MULT = mybir.AluOpType.mult
ADD = mybir.AluOpType.add

P = 128
PACK = 4
PASS = P * PACK
PASSES = D // PASS
GROUPS = B * T // PASS
PACKED = PACK * PASS
SCALES_PER_ROW = D // P
INV_SQRT_T = 1.0 / 32.0

W_LEAD = 14
X_LEAD = 22
TURN_DELAY = 6
FINISH_LAG = 4
STATE_LAG = 16


def tile_yocogatedretentionchunkstate_kernel(tc, x_bytes, x_scale, wk, wv, dec, beta, gamma, s_prev, out):
    nc = tc.nc
    with ExitStack() as ctx:
        keep = ctx.enter_context(tc.tile_pool(name="keep", bufs=1))
        work = ctx.enter_context(tc.tile_pool(name="work", bufs=1))
        psum = ctx.enter_context(tc.psum_pool(name="psum", bufs=8))
        ctx.enter_context(tc.manual_schedule())

        x_in, w_rows, s_in = {}, {}, {}

        def load_x(grp, pair):
            b, g = divmod(grp, 2)
            x_in[grp, pair] = keep.tile([P, 2, D], U8, name="xbytes_%d_%d" % (grp, pair))
            tokens = x_bytes[b, PASS * g : PASS * (g + 1), :].rearrange("(p t) d -> p t d", t=PACK)
            nc.sync.dma_start(out=x_in[grp, pair][:], in_=tokens[:, 2 * pair : 2 * pair + 2, :])

        def load_w(blk, g, c0, c1):
            weight, base = (wk, wv)[blk % 2], PASS * (blk // 2)
            w_rows[blk, g, c0] = keep.tile([P, PACK, c1 - c0], BF16, name="wrows_%d_%d_%d" % (blk, g, c0))
            src = weight[PASS * g : PASS * (g + 1), base + c0 : base + c1].rearrange("(p t) n -> p t n", t=PACK)
            nc.sync.dma_start(out=w_rows[blk, g, c0][:], in_=src)

        def load_s(b):
            s_in[b] = keep.tile([P, 2 * H, K], BF16, name="sprev_%d" % b)
            nc.sync.dma_start(out=s_in[b][:], in_=s_prev[b].rearrange("h (m p) j -> p (h m) j", p=P))

        scale_in = keep.tile([P, SCALES_PER_ROW], F32, name="scale_in")
        dec_in = keep.tile([P, GROUPS, PACK * H], BF16, name="dec_in")
        beta_in = keep.tile([P, GROUPS, PACK], BF16, name="beta_in")
        gamma_in = keep.tile([P, B * H], BF16, name="gamma_in")
        nc.sync.dma_start(out=scale_in[:], in_=x_scale.rearrange("a o (n m) -> n (a o m)", m=SCALES_PER_ROW))
        load_w(0, 0, 0, K)
        load_w(0, 0, K, PASS)
        load_x(0, 0)
        load_w(0, 1, 0, PASS)
        load_x(0, 1)
        nc.sync.dma_start(out=dec_in[:], in_=dec.rearrange("b (g p t) h -> p (b g) (t h)", p=P, t=PACK))
        load_w(1, 0, 0, PASS)
        load_w(1, 1, 0, PASS)
        nc.sync.dma_start(out=beta_in[:], in_=beta.rearrange("b (g p t) -> p (b g) t", p=P, t=PACK))
        load_x(1, 0)
        load_x(1, 1)
        for blk in (2, 3):
            for g in range(PASSES):
                load_w(blk, g, 0, PASS)
        nc.sync.dma_start(out=gamma_in[:], in_=gamma.rearrange("b h -> (b h)").partition_broadcast(P))
        load_s(0)
        for grp in (2, 3):
            load_x(grp, 0)
            load_x(grp, 1)
        load_s(1)

        ident_f32 = keep.tile([P, P], F32, name="ident_f32")
        make_identity(nc, ident_f32[:])
        ident_bf16 = keep.tile([P, P], BF16, name="ident_bf16")
        make_identity(nc, ident_bf16[:])

        scale_all = keep.tile([P, D], F32, name="scale_all")
        scale_by_m = scale_all[:].rearrange("p (n m) -> p n m", m=SCALES_PER_ROW)
        for m0 in range(0, SCALES_PER_ROW, PACK):
            bank = psum.tile([P, PASS], F32, name="bank")
            for m in range(PACK):
                column = scale_in[:, m0 + m : m0 + m + 1].to_broadcast([P, P])
                nc.tensor.transpose(bank[:, P * m : P * (m + 1)], column, ident_f32[:])
            nc.scalar.activation(
                out=scale_by_m[:, :, m0 : m0 + PACK], in_=bank[:].rearrange("p (m n) -> p n m", m=PACK), func=COPY
            )

        dec32 = keep.tile([P, GROUPS * PACK * H], F32, name="dec32")
        beta32 = keep.tile([P, GROUPS * PACK], F32, name="beta32")

        def widen_factors():
            nc.vector.tensor_copy(
                out=dec32[:].rearrange("p (g h t) -> p g h t", h=H, t=PACK),
                in_=dec_in[:].rearrange("p g (t h) -> p g h t", h=H),
            )
            nc.vector.tensor_scalar(
                out=beta32[:], in0=beta_in[:].rearrange("p g t -> p (g t)"), scalar1=INV_SQRT_T, scalar2=None, op0=MULT
            )

        def pack(copy, rows, packed):
            copy(
                out=packed.rearrange("p (c i t) -> p c t i", i=4, t=PACK),
                in_=rows.rearrange("p t (c i) -> p c t i", i=4),
            )

        def quantize(packed, pool, name, bufs):
            n = packed.shape[1] // PACK
            codes = pool.tile([P, n], U32, name=name + "_codes", bufs=bufs, align_bytes=64)
            scales = pool.tile([P, n], U8, name=name + "_scales", bufs=bufs, align_bytes=64)
            nc.vector.quantize_mx(out=codes[:].bitcast(FP8X4), scales=scales[:], in_=packed)
            return codes, scales

        def window(quantised, c0, c1):
            return quantised[0][:, c0:c1], quantised[1][:, c0:c1]

        def mx_sum(out_ap, lhs_by_pass, rhs_by_pass):
            for g, (lhs, rhs) in enumerate(zip(lhs_by_pass, rhs_by_pass)):
                nc.tensor.matmul_mx(
                    out=out_ap,
                    lhsT=lhs[0].bitcast(FP8X4),
                    lhsT_scale=lhs[1],
                    rhs=rhs[0].bitcast(FP8X4),
                    rhs_scale=rhs[1],
                    start=(g == 0),
                    stop=(g == len(lhs_by_pass) - 1),
                )

        w_packed, w_q = {}, {}

        def w_target(blk, g, c0, c1):
            if blk not in w_packed:
                w_packed[blk] = work.tile([P, PASSES * PACKED], BF16, name="w_packed", bufs=2, align_bytes=64)
            return w_packed[blk][:, PACKED * g + PACK * c0 : PACKED * g + PACK * c1]

        def pack_w(copy, blk, g, c0):
            rows = w_rows[blk, g, c0]
            pack(copy, rows[:], w_target(blk, g, c0, c0 + rows.shape[2]))

        def weave_w(blk, g, half):
            target = w_target(blk, g, K * half, K * (half + 1))
            bank = psum.tile([P, 2 * PASS], BF16, name="bank")
            for n in range(2):
                c0 = K * half + P * n
                nc.tensor.matmul(
                    bank[:, PASS * n : PASS * (n + 1)],
                    lhsT=ident_bf16[:],
                    rhs=w_rows[blk, g, 0][:, :, c0 : c0 + P].rearrange("p t n -> p n t"),
                    start=True,
                    stop=True,
                )
            nc.scalar.copy(out=target, in_=bank[:])

        def quantize_w(blk, passes):
            packed = w_packed[blk][:, PACKED * passes[0] : PACKED * (passes[-1] + 1)]
            quantised = quantize(packed, keep, "wq_%d_%d" % (blk, passes[0]), 1)
            for n, g in enumerate(passes):
                w_q[blk, g] = window(quantised, PASS * n, PASS * (n + 1))

        x_scaled, x_packed, x_q = {}, {}, {}

        def scale_x(grp, t):
            x_scaled[grp, t] = work.tile([P, D], BF16, name="x_scaled", bufs=6)
            values = x_in[grp, t // 2][:, t % 2, :].bitcast(FP8)
            nc.vector.tensor_tensor(out=x_scaled[grp, t][:], in0=values, in1=scale_all[:], op=MULT)

        def turn_x(grp, slots):
            banks = []
            for t in slots:
                words = x_scaled[grp, t][:].bitcast(F32)
                bank = psum.tile([P, PASS], F32, name="bank")
                for g in range(PASSES):
                    for u in range(2):
                        j = 2 * g + u
                        every_second = words[:, 2 * P * g + u : 2 * P * (g + 1) : 2]
                        nc.tensor.transpose(bank[:, P * j : P * (j + 1)], every_second, ident_f32[:])
                banks.append(bank)
            x_packed[grp, slots] = work.tile([P, D * len(slots)], BF16, name="x_packed", bufs=3, align_bytes=64)
            for n, bank in enumerate(banks):
                target = x_packed[grp, slots][:, D * n : D * (n + 1)].bitcast(F32)
                nc.scalar.copy(
                    out=target.rearrange("p (g r u) -> p g r u", g=PASSES, u=2),
                    in_=bank[:].rearrange("p (g u r) -> p g r u", g=PASSES, u=2),
                )

        def quantize_x(grp, slots):
            quantised = quantize(x_packed[grp, slots][:], work, "x_q", 8)
            for n, t in enumerate(slots):
                x_q[grp, t] = [window(quantised, P * (PASSES * n + g), P * (PASSES * n + g + 1)) for g in range(PASSES)]

        kv_rows, kv_packed, kv_q = {}, {}, {}

        def factor(grp, blk, hh, t):
            if blk % 2 == 0:
                col = (grp * H + blk + hh) * PACK + t
                return dec32[:, col : col + 1]
            return beta32[:, grp * PACK + t : grp * PACK + t + 1]

        def project(grp, blk, t):
            if t == 0:
                kv_rows[grp, blk] = work.tile([P, PACK, PASS], BF16, name="kv_rows", bufs=7)
            bank = psum.tile([P, PASS], F32, name="bank")
            mx_sum(bank[:], x_q[grp, t], [w_q[blk, g] for g in range(PASSES)])
            width = K if blk % 2 == 0 else PASS
            for hh in range(PASS // width):
                cols = slice(width * hh, width * (hh + 1))
                nc.scalar.activation(
                    out=kv_rows[grp, blk][:, t, cols], in_=bank[:, cols], func=COPY, scale=factor(grp, blk, hh, t)
                )

        def project_head(grp, blk, hh, pair):
            if pair == 0:
                kv_rows[grp, blk, hh] = work.tile([P, PACK, K], BF16, name="kv_rows", bufs=7)
            bank = psum.tile([P, PASS], F32, name="bank")
            weights = [window(w_q[blk, g], K * hh, K * (hh + 1)) for g in range(PASSES)]
            for n in range(2):
                mx_sum(bank[:, K * n : K * (n + 1)], x_q[grp, 2 * pair + n], weights)
            for n in range(2):
                t = 2 * pair + n
                nc.scalar.activation(
                    out=kv_rows[grp, blk, hh][:, t, :],
                    in_=bank[:, K * n : K * (n + 1)],
                    func=COPY,
                    scale=factor(grp, blk, hh, t),
                )

        def pack_kv(copy, key):
            rows = kv_rows[key]
            kv_packed[key] = work.tile([P, PACK * rows.shape[2]], BF16, name="kv_packed", bufs=3, align_bytes=64)
            pack(copy, rows[:], kv_packed[key][:])

        def quantize_kv(key):
            quantised = quantize(kv_packed[key][:], work, "kv_q", 10)
            heads = key[2:] if len(key) == 3 else range(2)
            for n, hh in enumerate(heads):
                kv_q[key[0], key[1], hh] = window(quantised, K * n, K * (n + 1))

        state_bank = {}

        def state(b, h, halves):
            blk, hh = 2 * (h // 2), h % 2
            state_bank[b, h, halves] = psum.tile([P, K * len(halves)], F32, name="bank")
            for n, m in enumerate(halves):
                keys = [window(kv_q[2 * b + g, blk, hh], P * m, P * (m + 1)) for g in range(2)]
                vals = [kv_q[2 * b + g, blk + 1, hh] for g in range(2)]
                mx_sum(state_bank[b, h, halves][:, K * n : K * (n + 1)], keys, vals)

        def blend(b, h, halves):
            first, count = halves[0], len(halves)
            res = work.tile([P, K * count], F32, name="res", bufs=5)
            previous = s_in[b][:, 2 * h + first : 2 * h + first + count, :].rearrange("p m j -> p (m j)")
            nc.vector.scalar_tensor_tensor(
                out=res[:],
                in0=previous,
                scalar=gamma_in[:, b * H + h : b * H + h + 1],
                in1=state_bank[b, h, halves][:],
                op0=MULT,
                op1=ADD,
            )
            stored = out[b, h, P * first : P * (first + count), :].rearrange("(m p) j -> p m j", p=P)
            nc.sync.dma_start(out=stored, in_=res[:].rearrange("p (m j) -> p m j", m=count))

        on_vector, on_scalar = nc.vector.tensor_copy, nc.scalar.copy
        both = (0, 1)

        units = [(g, 2 * hp + kind) for hp in range(2) for g in range(2) for kind in range(2)]
        units = units + [(grp, blk) for grp in (2, 3) for blk in range(4)]
        first_tick_of_group = {grp: PACK * [u[0] for u in units].index(grp) for grp in range(GROUPS)}
        first_tick_of_block = {blk: PACK * [u[1] for u in units].index(blk) for blk in range(4)}
        last = len(units) - 1

        pack_w(on_vector, 0, 0, 0)
        pack_w(on_vector, 0, 0, K)
        pack_w(on_scalar, 0, 1, 0)
        quantize_w(0, (0,))
        scale_x(0, 0)
        scale_x(0, 1)
        turn_x(0, (0,))
        quantize_w(0, (1,))
        scale_x(0, 2)
        quantize_x(0, (0,))
        widen_factors()
        turn_x(0, (1,))
        pack_w(on_scalar, 1, 1, 0)
        scale_x(0, 3)
        quantize_x(0, (1,))
        pack_w(on_vector, 1, 0, 0)

        plan = {}

        def at(tick, job, *args):
            plan.setdefault(tick, []).append((job, args))

        for t in (2, 3):
            at(t - 2, turn_x, 0, (t,))
            at(t - 1, quantize_x, 0, (t,))
        at(1, quantize_w, 1, both)

        woven = {2: (1,), 3: both}
        at(first_tick_of_block[2] - W_LEAD + 2, pack_w, on_vector, 2, 0, 0)
        for blk in (2, 3):
            halves_to_weave = [(g, half) for g in woven[blk] for half in range(2)]
            for n, (g, half) in enumerate(halves_to_weave):
                at(first_tick_of_block[blk] - W_LEAD + 2 * n, weave_w, blk, g, half)
            at(first_tick_of_block[blk] - PACK, quantize_w, blk, both)

        for grp in range(1, GROUPS):
            start, step, delay = (2, 1, 2) if grp == 1 else (first_tick_of_group[grp] - X_LEAD, PACK, TURN_DELAY)
            for t in range(PACK):
                at(start + step * t, scale_x, grp, t)
            for t in (0, 2):
                turn = start + step * (t + 1) + delay
                at(turn, turn_x, grp, (t, t + 1))
                at(turn + 2, quantize_x, grp, (t, t + 1))

        for u, (grp, blk) in enumerate(units[:last]):
            for t in range(PACK):
                at(PACK * u + t, project, grp, blk, t)

        for u, (grp, blk) in enumerate(units[: last - 1]):
            done = PACK * u + PACK - 1 + FINISH_LAG
            at(done, pack_kv, on_vector, (grp, blk))
            if grp < GROUPS - 1:
                at(done + PACK + 1, quantize_kv, (grp, blk))
            if grp == 1 and blk % 2 == 1:
                for h in (blk - 1, blk):
                    at(done + STATE_LAG, state, 0, h, both)
                    at(done + STATE_LAG + 1, blend, 0, h, both)

        for tick in sorted(plan):
            for job, args in plan[tick]:
                job(*args)

        grp = GROUPS - 1
        quantize_kv((grp, 0))
        project_head(grp, 3, 0, 0)
        project_head(grp, 3, 0, 1)
        project_head(grp, 3, 1, 0)
        pack_kv(on_vector, (grp, 2))
        project_head(grp, 3, 1, 1)
        quantize_kv((grp, 1))
        pack_kv(on_vector, (grp, 3, 0))
        quantize_kv((grp, 2))
        quantize_kv((grp, 3, 0))
        pack_kv(on_scalar, (grp, 3, 1))
        for h in range(2):
            state(1, h, both)
        for h in range(2):
            blend(1, h, both)
        quantize_kv((grp, 3, 1))
        state(1, 2, both)
        blend(1, 2, both)
        for m in range(2):
            state(1, 3, (m,))
        for m in range(2):
            blend(1, 3, (m,))
